import numpy as np, ml_dtypes
CORES = [8,9,10,11,12,13]
N = 6
import mx_ref
BF = ml_dtypes.bfloat16
def entries(a):
    return np.ascontiguousarray(a.T).reshape(-1)
def table(e):
    return np.ascontiguousarray(np.reshape(e, (-1, 16)).T).astype(np.int32)
def cols(t, e):
    v = np.concatenate([t.reshape(128, -1, 4), np.zeros((128, 1, 4), BF)], axis=1)
    return np.ascontiguousarray(v[:, e]).reshape(128, -1)
def f(rng, *shape):
    return mx_ref.flush((rng.standard_normal(shape, dtype=np.float32) * np.exp2(rng.integers(-2, 3, shape[:-1] + (1,)))).astype(BF))
def wide(rng, *shape, cols=0):
    v = rng.standard_normal(shape, dtype=np.float32) * np.exp2(rng.integers(-12, 13, shape)).astype(np.float32)
    if cols: v *= np.repeat(np.exp2(rng.integers(-cols, cols + 1, shape[:-2] + (1, shape[-1] // 4))) * (rng.random(shape[:-2] + (1, shape[-1] // 4)) > 0.0625), 4, axis=-1).astype(np.float32)
    return mx_ref.flush(v.astype(BF))
B, K, O = 256, 96, 3
def order(r):
    return [(r + 1 + i) % N for i in range(N)]
def some(rng, where, n):
    e = np.full(K, -1); e[rng.permutation(K)[:n]] = rng.permutation(where)[:n]
    return table(e)
def setup_inputs(rng):
    return {"b": f(rng, N, 128, 4 * B), "x": f(rng, N, 128, 4 * K), "w": f(rng, N, 128, 512 * O), "pl": np.stack([some(rng, np.arange(B), int(rng.integers(K >> 1, K + 1))) for r in range(N)])}
def setup_inputs_same(rng):
    d = setup_inputs(rng)
    for i in range(50):
        at = rng.permutation(B)[:K]; quiet = rng.permutation(N)[:int(rng.integers(1, 3))].tolist()
        pl = [some(rng, at, 0 if r in quiet else int(rng.integers(K >> 2, (3 * K >> 2) + 1))) for r in range(N)]
        s = [set(entries(pl[r]).tolist()) - {-1} for r in range(N) if r not in quiet]
        if all(s[j] & s[k] for j in range(len(s)) for k in range(j)):
            d["pl"] = np.stack(pl); return d
    raise RuntimeError("no draw in which any two of the writing ranks have a place in common")
def setup_inputs_apart(rng):
    d = setup_inputs(rng); at, start = rng.permutation(B), int(rng.integers(N))
    pl = [None] * N
    for i in range(N):
        e = at[K * i:K * i + K]
        pl[(start + i) % N] = some(rng, e, len(e))
    d["pl"] = np.stack(pl); return d
def setup_inputs_runs(rng):
    d = setup_inputs(rng); p = rng.permutation(N)
    pl = [None] * N
    for i in range(N):
        if i == 0: at = np.arange(0)
        elif i % 3 == 1: at = (int(rng.integers(B)) + np.arange(K)) % B
        elif i % 3 == 2: at = np.flatnonzero(np.isin(np.arange(B) % 8, rng.permutation(8)[:8 * K // B]))
        else: at = rng.permutation(B)[:K - int(rng.integers(K >> 2, (3 * K >> 2) + 1))]
        at = rng.permutation(at); a = int(rng.integers(len(at) + 1))
        pl[p[i]] = table(np.concatenate([at[:a], np.full(K - len(at), -1), at[a:]]))
    d["pl"] = np.stack(pl); return d
def setup_inputs_halves(rng):
    d = setup_inputs(rng); at, start = rng.permutation(B), int(rng.integers(N))
    pl = [None] * N
    for i in range(N): pl[(start + i) % N] = some(rng, at[:B >> 1] if i < N >> 1 else at[B >> 1:], K)
    d["pl"] = np.stack(pl); return d
def setup_inputs_spread(rng):
    d = setup_inputs(rng); d["b"] = wide(rng, N, 128, 4 * B, cols=6); d["x"] = wide(rng, N, 128, 4 * K, cols=6); return d
def check_inputs(d):
    bad = []
    for r in range(N):
        e = entries(d["pl"][r])
        if e.min() < -1 or e.max() >= B: bad.append("pl")
        e = e[e >= 0]
        if len(set(e.tolist())) != len(e): bad.append("pl names a place twice")
    return bad
def reference(b, x, w, pl):
    y = np.zeros((N, 128, O * B), np.float32)
    for r in range(N):
        m = np.array(b[r]).reshape(128, B, 4)
        for s in order(r):
            e = entries(pl[s]); k = np.flatnonzero(e >= 0)
            m[:, e[k]] = x[s].reshape(128, K, 4)[:, k]
        q = mx_ref.quantize(m.reshape(128, 4 * B))
        for o in range(O):
            y[r][:, B * o:B * o + B] = mx_ref.matmul(mx_ref.quantize(cols(w[r], np.arange(128 * o, 128 * o + 128))), q)
    return {"y": y}

@@ -1,0 +1,217 @@
+from concourse.bass import DstId, RemoteDMATransfer
+from concourse.mybir import dt, AluOpType, ActivationFunctionType
+
+N, B, K, O = 6, 256, 96, 3
+OWN = B + K * (N - 1)
+WIDE = OWN + K
+ALL = OWN + 128
+DUM = 16
+
+
+def slot(d):
+    return B + K * (N - 1 - d)
+
+
+SCRATCH = {
+    "xt": ("sbuf", [128, 512], "bfloat16"),
+    "bt": ("sbuf", [128, 4 * B], "bfloat16"),
+    "wt": ("sbuf", [128, 512 * O], "bfloat16"),
+    "q": ("sbuf", [128, ALL], "float8_e4m3fn_x4"),
+    "sq": ("sbuf", [128, ALL], "uint8"),
+    "wq": ("sbuf", [128, 128 * O], "float8_e4m3fn_x4"),
+    "wsq": ("sbuf", [128, 128 * O], "uint8"),
+    "m": ("sbuf", [128, B], "float8_e4m3fn_x4"),
+    "ms": ("sbuf", [128, B], "uint8"),
+    "ys": ("sbuf", [128, O * B], "float32"),
+    "ps": ("psum", [128, 2048], "float32"),
+    "own": ("sbuf", [128, 4], "int32"),
+    "land": ("sbuf", [128, N - 1], "int32"),
+    "neg": ("sbuf", [128, 8], "float32"),
+    "dst": ("sbuf", [128, 8], "int32"),
+    "nego": ("sbuf", [128, 4], "float32"),
+    "off": ("sbuf", [128, 2 * N], "uint16"),
+    "offo": ("sbuf", [128, 2], "uint16"),
+    "pi": ("sbuf", [128, 1], "int32"),
+    "lo": ("sbuf", [128, 1], "int32"),
+    "lof": ("sbuf", [128, 1], "float32"),
+    "dcol": ("sbuf", [128, 1], "float32"),
+    "m0": ("sbuf", [128, 1], "float32"),
+    "m1": ("sbuf", [128, 1], "float32"),
+    "qf": ("sbuf", [128, 16], "float32"),
+    "qn": ("sbuf", [128, 16], "float32"),
+    "ni": ("sbuf", [128, 16], "int32"),
+    "nf": ("sbuf", [128, 16], "float32"),
+    "kq": ("sbuf", [128, 16], "float32"),
+    "kv": ("sbuf", [128, 16], "float32"),
+    "val": ("sbuf", [128, 16 * N], "float32"),
+    "win": ("sbuf", [128, B + DUM], "float32"),
+    "tt": ("sbuf", [128, B], "float32"),
+    "l1": ("sbuf", [128, 16], "float32"),
+    "l2": ("sbuf", [128, 16], "float32"),
+    "l3": ("sbuf", [128, 8], "float32"),
+    "in2": ("sbuf", [128, 32], "float32"),
+    "t2": ("sbuf", [128, 32], "float32"),
+    "e2": ("sbuf", [128, 32], "float32"),
+    "f2": ("sbuf", [128, 32], "float32"),
+    "pick": ("sbuf", [128, 16], "uint16"),
+}
+SEMAPHORES = ["sx", "sb", "sw", "sp", "mo", "gi", "v", "qx", "qb", "qw", "al", "ac", "asc", "loc", "offr", "pkv", "pks",
+              "mm0", "mm1", "mm2", "mm3", "c0", "c1", "c2", "c3", "sy"]
+
+
+def rank_program(g, core, T, topo):
+    r = T.rank_of(core)
+    if r is None:
+        return
+    A, s = AluOpType, T.sem
+    V, S, P, Y = g.vector, g.scalar, g.tensor, g.sync
+    Copy = ActivationFunctionType.Copy
+
+    S.dma_start(T.own[0:96, 0:1], T.pl[:]).then_inc(s.sp, 16)
+    Y.dma_start(T.xt[:, 0:4 * K], T.x[:]).then_inc(s.sx, 16)
+    Y.dma_start(T.bt[:], T.b[:]).then_inc(s.sb, 16)
+    S.dma_start(T.wt[:], T.w[:]).then_inc(s.sw, 16)
+
+    n = [0]
+
+    def v(ins):
+        n[0] += 1
+        return ins.then_inc(s.v, 1)
+
+    def vw():
+        V.wait_ge(s.v, n[0])
+
+    V.memset(T.own[96:128, 0:1], -1).then_inc(s.mo, 1)
+    v(V.memset(T.xt[:, 4 * K:512], 0.0))
+    v(V.memset(T.in2[:], 0.0))
+
+    g.iota(T.pi[:], [[0, 1]], 0, 1).then_inc(s.gi, 1)
+    g.iota(T.qf[:], [[1, 16]], 0, 1, allow_small_or_imprecise_dtypes=True).then_inc(s.gi, 1)
+    g.iota(T.win[:], [[1, B + DUM]], 0, 0, allow_small_or_imprecise_dtypes=True).then_inc(s.gi, 1)
+
+    others = [(r + 1 + i) % N for i in range(N - 1)]
+    ids, mask = [], None
+    for o in others:
+        rid, pid, _se = topo.addr(T.cores[o])
+        ids.append(DstId(rid=rid, pnc=pid))
+        k = topo.mask(core, T.cores[o])
+        mask = k if mask is None else mask & k
+    eng = len([e for e in topo.engines(core, T.cores[others[0]])])
+
+    def send(src, dsts, sem):
+        g.remote_dma_fused([RemoteDMATransfer(dst_ids=ids, dma_engine_mask=mask, remote_sem=sem, srcs=[src], dsts=dsts)],
+                           local_sem=s.loc)
+
+    ds = [(o - r) % N for o in others]
+    g.wait_ge(s.sp, 16)
+    g.wait_ge(s.mo, 1)
+    send(T.own[:, 0:1], [T.land[:, N - 1 - d:N - d] for d in ds], s.al)
+    g.wait_ge(s.qx, 1)
+    send(T.q[:, OWN:WIDE].bitcast(dt.uint8), [T.q[:, slot(d):slot(d) + K].bitcast(dt.uint8) for d in ds], s.ac)
+    send(T.sq[:, OWN:WIDE], [T.sq[:, slot(d):slot(d) + K] for d in ds], s.asc)
+
+    V.wait_ge(s.gi, 3)
+    v(V.tensor_scalar(T.lo[:], T.pi[:], 15, None, A.bitwise_and))
+    v(V.tensor_scalar(T.m0[:], T.pi[:], 16, None, A.is_lt))
+    v(V.tensor_scalar(T.m1[:], T.pi[:], 16, None, A.is_ge))
+    vw()
+    v(V.tensor_copy(T.lof[:], T.lo[:]))
+    v(V.tensor_scalar(T.dcol[:], T.lo[:], B + 1.0, None, A.add))
+    vw()
+    v(V.tensor_scalar(T.qn[:], T.qf[:], T.lof[:], None, A.subtract))
+    vw()
+    v(V.tensor_scalar(T.nf[:], T.qn[:], 1.0 / 6, -5.0 / 12, A.mult, A.add))
+    v(V.tensor_scalar(T.kq[:], T.qn[:], 16.0, None, A.mult))
+    vw()
+    v(V.tensor_copy(T.ni[:], T.nf[:]))
+    vw()
+    v(V.tensor_scalar(T.qf[:], T.ni[:], 95.0, None, A.mult))
+    vw()
+    v(V.tensor_tensor(T.kv[:], T.kq[:], T.qf[:], A.subtract))
+    vw()
+    for j in range(N):
+        v(V.tensor_scalar(T.val[:, 16 * j:16 * j + 16], T.kv[:], float(slot(N - 1 - j)), None, A.add))
+
+    vw()
+    V.wait_ge(s.sx, 16)
+    V.quantize_mx(T.q[:, OWN:ALL], T.sq[:, OWN:ALL], T.xt[:]).then_inc(s.qx, 1)
+    V.wait_ge(s.sp, 16)
+    V.wait_ge(s.mo, 1)
+    v(V.tensor_scalar(T.nego[:, 0:1], T.own[:, 0:1], 0.0, T.dcol[:], A.is_lt, A.mult))
+    vw()
+    v(V.tensor_scalar(T.offo[:, 0:1], T.own[:, 0:1], T.nego[:, 0:1], None, A.add))
+    V.wait_ge(s.sb, 16)
+    V.quantize_mx(T.q[:, 0:B], T.sq[:, 0:B], T.bt[:]).then_inc(s.qb, 1)
+    V.wait_ge(s.sw, 16)
+    V.quantize_mx(T.wq[:], T.wsq[:], T.wt[:]).then_inc(s.qw, 1)
+
+    V.wait_ge(s.al, eng * (N - 1))
+    v(V.tensor_scalar(T.neg[:, 0:N - 1], T.land[:], 0.0, T.dcol[:], A.is_lt, A.mult))
+    vw()
+    v(V.tensor_tensor(T.dst[:, 0:N - 1], T.land[:], T.neg[:, 0:N - 1], A.add))
+    vw()
+    v(V.tensor_copy(T.off[:, 0:2 * (N - 1):2], T.dst[:, 0:N - 1]))
+    vw()
+    for j in range(N):
+        o = T.off[:, 2 * j:2 * j + 1] if j < N - 1 else T.offo[:, 0:1]
+        v(V.tensor_copy(T.win[:].indirect(o), T.val[:, 16 * j:16 * j + 16]))
+        vw()
+    v(V.transpose(T.tt[:], T.win[:, 0:B]))
+    vw()
+    v(V.tensor_tensor(T.l1[0:64, :], T.tt[0:64, 0:B:16], T.tt[64:128, 0:B:16], A.max))
+    vw()
+    v(V.tensor_tensor(T.l2[0:32, :], T.l1[0:32, :], T.l1[32:64, :], A.max))
+    vw()
+    v(V.tensor_tensor(T.l3[0:32, :], T.l2[0:32, 0:16:2], T.l2[0:32, 1:16:2], A.max))
+    vw()
+    v(V.tensor_scalar(T.in2[0:32, 0:16:2], T.l3[0:32, :], T.m0[0:32, :], None, A.mult))
+    v(V.tensor_scalar(T.in2[0:32, 1:16:2], T.l3[0:32, :], T.m1[0:32, :], None, A.mult))
+    vw()
+    v(V.transpose(T.t2[0:32, :], T.in2[0:32, :]))
+    vw()
+    v(V.tensor_tensor(T.e2[0:32, 0:16], T.t2[0:32, 0:16], T.t2[0:32, 16:32], A.max))
+    v(V.tensor_tensor(T.e2[0:32, 16:32], T.t2[0:32, 0:16], T.t2[0:32, 16:32], A.max))
+    vw()
+    v(V.transpose(T.f2[0:32, :], T.e2[0:32, :]))
+    vw()
+    for a in range(4):
+        V.tensor_copy(T.pick[32 * a:32 * a + 32, :], T.f2[0:32, 0:16]).then_inc(s.offr, 1)
+
+    V.wait_ge(s.offr, 4)
+    V.wait_ge(s.qx, 1)
+    V.wait_ge(s.qb, 1)
+    V.wait_ge(s.ac, eng * (N - 1))
+    for h in range(2):
+        V.tensor_copy(T.m[:, 128 * h:128 * h + 128].bitcast(dt.uint32),
+                      T.q[:, 0:WIDE].bitcast(dt.uint32).indirect(T.pick[:, 8 * h:8 * h + 8])).then_inc(s.pkv, 1)
+    V.wait_ge(s.asc, eng * (N - 1))
+    V.tensor_copy(T.ms[:, 0:128], T.sq[:, 0:WIDE].indirect(T.pick[:, 0:8])).then_inc(s.pkv, 1)
+    S.wait_ge(s.qx, 1)
+    S.wait_ge(s.qb, 1)
+    S.wait_ge(s.offr, 4)
+    S.wait_ge(s.asc, eng * (N - 1))
+    S.activation(T.ms[:, 128:256], T.sq[:, 0:WIDE].indirect(T.pick[:, 8:16]), Copy).then_inc(s.pks, 1)
+
+    P.wait_ge(s.qw, 1)
+    P.wait_ge(s.pkv, 3)
+    P.wait_ge(s.pks, 1)
+    parts = [(0, 0, 256, V), (1, 0, 256, S), (2, 0, 128, V), (2, 128, 128, S)]
+    for i in range(4):
+        o, a, w, _ = parts[i]
+        P.matmul_mx(T.ps[:, 512 * i:512 * i + w], T.wq[:, 128 * o:128 * o + 128], T.wsq[:, 128 * o:128 * o + 128],
+                    T.m[:, a:a + w], T.ms[:, a:a + w], True, True).then_inc(s["mm%d" % i], 1)
+    for i in range(4):
+        o, a, w, e = parts[i]
+        e.wait_ge(s["mm%d" % i], 1)
+        out, src = T.ys[:, 256 * o + a:256 * o + a + w], T.ps[:, 512 * i:512 * i + w]
+        (V.tensor_copy(out, src) if e is V else S.activation(out, src, Copy)).then_inc(s["c%d" % i], 1)
+    Y.wait_ge(s.c0, 1)
+    Y.dma_start(T.y[:, 0:256], T.ys[:, 0:256]).then_inc(s.sy, 16)
+    Y.wait_ge(s.c1, 1)
+    Y.dma_start(T.y[:, 256:512], T.ys[:, 256:512]).then_inc(s.sy, 16)
+    Y.wait_ge(s.c2, 1)
+    Y.wait_ge(s.c3, 1)
+    Y.dma_start(T.y[:, 512:768], T.ys[:, 512:768]).then_inc(s.sy, 16)
+    Y.wait_ge(s.sy, 48)
+    V.wait_ge(s.v, n[0])
+    g.wait_ge(s.loc, 3 * eng)

@@ -25,11 +25,8 @@ SCRATCH = {
     "ys": ("sbuf", [128, O * B], "float32"),
     "ps": ("psum", [128, 2048], "float32"),
     "own": ("sbuf", [128, 4], "int32"),
-    "land": ("sbuf", [128, N - 1], "int32"),
-    "neg": ("sbuf", [128, 8], "float32"),
-    "dst": ("sbuf", [128, 8], "int32"),
+    "land": ("sbuf", [128, 2 * (N - 1)], "uint16"),
     "nego": ("sbuf", [128, 4], "float32"),
-    "off": ("sbuf", [128, 2 * N], "uint16"),
     "offo": ("sbuf", [128, 2], "uint16"),
     "pi": ("sbuf", [128, 1], "int32"),
     "lo": ("sbuf", [128, 1], "int32"),
@@ -55,8 +52,8 @@ SCRATCH = {
     "f2": ("sbuf", [128, 32], "float32"),
     "pick": ("sbuf", [128, 16], "uint16"),
 }
-SEMAPHORES = ["sx", "sb", "sw", "sp", "mo", "gi", "v", "qx", "qb", "qw", "al", "ac", "asc", "loc", "offr", "pkv", "pks",
-              "mm0", "mm1", "mm2", "mm3", "c0", "c1", "c2", "c3", "sy"]
+SEMAPHORES = ["sx", "sb", "sw", "sw2", "gw", "sp", "mo", "gi", "gn", "v", "qx", "qb", "qw0", "qw1", "qw2", "al", "ac", "asc", "loc",
+              "ofs", "offr", "pkv", "pks", "mm0", "mm1", "mm2", "mm3", "c0", "c1", "c2", "c3", "sy"]
 
 
 def rank_program(g, core, T, topo):
@@ -70,7 +67,9 @@ def rank_program(g, core, T, topo):
     S.dma_start(T.own[0:96, 0:1], T.pl[:]).then_inc(s.sp, 16)
     Y.dma_start(T.xt[:, 0:4 * K], T.x[:]).then_inc(s.sx, 16)
     Y.dma_start(T.bt[:], T.b[:]).then_inc(s.sb, 16)
-    S.dma_start(T.wt[:], T.w[:]).then_inc(s.sw, 16)
+    S.dma_start(T.wt[:, 0:512], T.w[:, 0:512]).then_inc(s.sw, 16)
+    Y.wait_ge(s.gw, 1)
+    Y.dma_start(T.wt[:, 512:1536], T.w[:, 512:1536]).then_inc(s.sw2, 16)
 
     n = [0]
 
@@ -81,13 +80,9 @@ def rank_program(g, core, T, topo):
     def vw():
         V.wait_ge(s.v, n[0])
 
-    V.memset(T.own[96:128, 0:1], -1).then_inc(s.mo, 1)
-    v(V.memset(T.xt[:, 4 * K:512], 0.0))
-    v(V.memset(T.in2[:], 0.0))
-
     g.iota(T.pi[:], [[0, 1]], 0, 1).then_inc(s.gi, 1)
-    g.iota(T.qf[:], [[1, 16]], 0, 1, allow_small_or_imprecise_dtypes=True).then_inc(s.gi, 1)
-    g.iota(T.win[:], [[1, B + DUM]], 0, 0, allow_small_or_imprecise_dtypes=True).then_inc(s.gi, 1)
+    g.iota(T.qf[:], [[1, 16]], 0, 1, allow_small_or_imprecise_dtypes=True).then_inc(s.gn, 1)
+    g.iota(T.win[:], [[1, B + DUM]], 0, 0, allow_small_or_imprecise_dtypes=True).then_inc(s.gn, 1)
 
     others = [(r + 1 + i) % N for i in range(N - 1)]
     ids, mask = [], None
@@ -103,21 +98,33 @@ def rank_program(g, core, T, topo):
                            local_sem=s.loc)
 
     ds = [(o - r) % N for o in others]
-    g.wait_ge(s.sp, 16)
-    g.wait_ge(s.mo, 1)
-    send(T.own[:, 0:1], [T.land[:, N - 1 - d:N - d] for d in ds], s.al)
+    g.wait_ge(s.ofs, 1)
+    send(T.offo[:, 0:1], [T.land[:, 2 * (N - 1 - d):2 * (N - 1 - d) + 1] for d in ds], s.al)
     g.wait_ge(s.qx, 1)
     send(T.q[:, OWN:WIDE].bitcast(dt.uint8), [T.q[:, slot(d):slot(d) + K].bitcast(dt.uint8) for d in ds], s.ac)
     send(T.sq[:, OWN:WIDE], [T.sq[:, slot(d):slot(d) + K] for d in ds], s.asc)
+    g.sem_inc(s.gw, 1)
 
-    V.wait_ge(s.gi, 3)
+    V.memset(T.own[96:128, 0:1], -1).then_inc(s.mo, 1)
+    v(V.memset(T.xt[:, 4 * K:512], 0.0))
+    v(V.memset(T.in2[:], 0.0))
+    V.wait_ge(s.gi, 1)
     v(V.tensor_scalar(T.lo[:], T.pi[:], 15, None, A.bitwise_and))
     v(V.tensor_scalar(T.m0[:], T.pi[:], 16, None, A.is_lt))
     v(V.tensor_scalar(T.m1[:], T.pi[:], 16, None, A.is_ge))
     vw()
-    v(V.tensor_copy(T.lof[:], T.lo[:]))
     v(V.tensor_scalar(T.dcol[:], T.lo[:], B + 1.0, None, A.add))
+    v(V.tensor_copy(T.lof[:], T.lo[:]))
     vw()
+    V.wait_ge(s.mo, 1)
+    V.wait_ge(s.sp, 16)
+    v(V.tensor_scalar(T.nego[:, 0:1], T.own[:, 0:1], 0.0, T.dcol[:], A.is_lt, A.mult))
+    vw()
+    V.tensor_scalar(T.offo[:, 0:1], T.own[:, 0:1], T.nego[:, 0:1], None, A.add).then_inc(s.ofs, 1)
+    V.wait_ge(s.sx, 16)
+    V.quantize_mx(T.q[:, OWN:ALL], T.sq[:, OWN:ALL], T.xt[:]).then_inc(s.qx, 1)
+
+    V.wait_ge(s.gn, 2)
     v(V.tensor_scalar(T.qn[:], T.qf[:], T.lof[:], None, A.subtract))
     vw()
     v(V.tensor_scalar(T.nf[:], T.qn[:], 1.0 / 6, -5.0 / 12, A.mult, A.add))
@@ -131,29 +138,16 @@ def rank_program(g, core, T, topo):
     vw()
     for j in range(N):
         v(V.tensor_scalar(T.val[:, 16 * j:16 * j + 16], T.kv[:], float(slot(N - 1 - j)), None, A.add))
-
-    vw()
-    V.wait_ge(s.sx, 16)
-    V.quantize_mx(T.q[:, OWN:ALL], T.sq[:, OWN:ALL], T.xt[:]).then_inc(s.qx, 1)
-    V.wait_ge(s.sp, 16)
-    V.wait_ge(s.mo, 1)
-    v(V.tensor_scalar(T.nego[:, 0:1], T.own[:, 0:1], 0.0, T.dcol[:], A.is_lt, A.mult))
-    vw()
-    v(V.tensor_scalar(T.offo[:, 0:1], T.own[:, 0:1], T.nego[:, 0:1], None, A.add))
     V.wait_ge(s.sb, 16)
     V.quantize_mx(T.q[:, 0:B], T.sq[:, 0:B], T.bt[:]).then_inc(s.qb, 1)
     V.wait_ge(s.sw, 16)
-    V.quantize_mx(T.wq[:], T.wsq[:], T.wt[:]).then_inc(s.qw, 1)
+    V.quantize_mx(T.wq[:, 0:128], T.wsq[:, 0:128], T.wt[:, 0:512]).then_inc(s.qw0, 1)
 
+    vw()
+    V.wait_ge(s.ofs, 1)
     V.wait_ge(s.al, eng * (N - 1))
-    v(V.tensor_scalar(T.neg[:, 0:N - 1], T.land[:], 0.0, T.dcol[:], A.is_lt, A.mult))
-    vw()
-    v(V.tensor_tensor(T.dst[:, 0:N - 1], T.land[:], T.neg[:, 0:N - 1], A.add))
-    vw()
-    v(V.tensor_copy(T.off[:, 0:2 * (N - 1):2], T.dst[:, 0:N - 1]))
-    vw()
     for j in range(N):
-        o = T.off[:, 2 * j:2 * j + 1] if j < N - 1 else T.offo[:, 0:1]
+        o = T.land[:, 2 * j:2 * j + 1] if j < N - 1 else T.offo[:, 0:1]
         v(V.tensor_copy(T.win[:].indirect(o), T.val[:, 16 * j:16 * j + 16]))
         vw()
     v(V.transpose(T.tt[:], T.win[:, 0:B]))
@@ -177,27 +171,27 @@ def rank_program(g, core, T, topo):
     for a in range(4):
         V.tensor_copy(T.pick[32 * a:32 * a + 32, :], T.f2[0:32, 0:16]).then_inc(s.offr, 1)
 
-    V.wait_ge(s.offr, 4)
     V.wait_ge(s.qx, 1)
     V.wait_ge(s.qb, 1)
     V.wait_ge(s.ac, eng * (N - 1))
-    for h in range(2):
-        V.tensor_copy(T.m[:, 128 * h:128 * h + 128].bitcast(dt.uint32),
-                      T.q[:, 0:WIDE].bitcast(dt.uint32).indirect(T.pick[:, 8 * h:8 * h + 8])).then_inc(s.pkv, 1)
-    V.wait_ge(s.asc, eng * (N - 1))
-    V.tensor_copy(T.ms[:, 0:128], T.sq[:, 0:WIDE].indirect(T.pick[:, 0:8])).then_inc(s.pkv, 1)
+    V.wait_ge(s.offr, 4)
+    V.tensor_copy(T.m[:].bitcast(dt.uint32), T.q[:, 0:WIDE].bitcast(dt.uint32).indirect(T.pick[:])).then_inc(s.pkv, 1)
     S.wait_ge(s.qx, 1)
     S.wait_ge(s.qb, 1)
-    S.wait_ge(s.offr, 4)
     S.wait_ge(s.asc, eng * (N - 1))
-    S.activation(T.ms[:, 128:256], T.sq[:, 0:WIDE].indirect(T.pick[:, 8:16]), Copy).then_inc(s.pks, 1)
+    S.wait_ge(s.offr, 4)
+    S.activation(T.ms[:], T.sq[:, 0:WIDE].indirect(T.pick[:]), Copy).then_inc(s.pks, 1)
+    V.wait_ge(s.sw2, 16)
+    for o in (1, 2):
+        V.quantize_mx(T.wq[:, 128 * o:128 * o + 128], T.wsq[:, 128 * o:128 * o + 128],
+                      T.wt[:, 512 * o:512 * o + 512]).then_inc(s["qw%d" % o], 1)
 
-    P.wait_ge(s.qw, 1)
-    P.wait_ge(s.pkv, 3)
+    P.wait_ge(s.pkv, 1)
     P.wait_ge(s.pks, 1)
-    parts = [(0, 0, 256, V), (1, 0, 256, S), (2, 0, 128, V), (2, 128, 128, S)]
+    parts = [(0, 0, 256, S), (1, 0, 256, V), (2, 0, 128, S), (2, 128, 128, V)]
     for i in range(4):
         o, a, w, _ = parts[i]
+        P.wait_ge(s["qw%d" % o], 1)
         P.matmul_mx(T.ps[:, 512 * i:512 * i + w], T.wq[:, 128 * o:128 * o + 128], T.wsq[:, 128 * o:128 * o + 128],
                     T.m[:, a:a + w], T.ms[:, a:a + w], True, True).then_inc(s["mm%d" % i], 1)
     for i in range(4):

@@ -5,7 +5,8 @@ N, B, K, O = 6, 256, 96, 3
 OWN = B + K * (N - 1)
 WIDE = OWN + K
 ALL = OWN + 128
-DUM = 16
+DUM = B + 96
+NONE = -1024.0
 
 
 def slot(d):
@@ -24,36 +25,33 @@ SCRATCH = {
     "ms": ("sbuf", [128, B], "uint8"),
     "ys": ("sbuf", [128, O * B], "float32"),
     "ps": ("psum", [128, 2048], "float32"),
-    "own": ("sbuf", [128, 4], "int32"),
-    "land": ("sbuf", [128, 2 * (N - 1)], "uint16"),
-    "nego": ("sbuf", [128, 4], "float32"),
-    "offo": ("sbuf", [128, 2], "uint16"),
-    "pi": ("sbuf", [128, 1], "int32"),
-    "lo": ("sbuf", [128, 1], "int32"),
-    "lof": ("sbuf", [128, 1], "float32"),
-    "dcol": ("sbuf", [128, 1], "float32"),
-    "m0": ("sbuf", [128, 1], "float32"),
-    "m1": ("sbuf", [128, 1], "float32"),
-    "qf": ("sbuf", [128, 16], "float32"),
-    "qn": ("sbuf", [128, 16], "float32"),
-    "ni": ("sbuf", [128, 16], "int32"),
-    "nf": ("sbuf", [128, 16], "float32"),
-    "kq": ("sbuf", [128, 16], "float32"),
-    "kv": ("sbuf", [128, 16], "float32"),
-    "val": ("sbuf", [128, 16 * N], "float32"),
-    "win": ("sbuf", [128, B + DUM], "float32"),
-    "tt": ("sbuf", [128, B], "float32"),
-    "l1": ("sbuf", [128, 16], "float32"),
-    "l2": ("sbuf", [128, 16], "float32"),
-    "l3": ("sbuf", [128, 8], "float32"),
+    "own": ("sbuf", [128, 3], "int32"),
+    "nd": ("sbuf", [128, 3], "int32"),
+    "sh": ("sbuf", [128, 1], "float32"),
+    "u": ("sbuf", [128, 3], "int32"),
+    "vd": ("sbuf", [128, 3], "int32"),
+    "off": ("sbuf", [128, 4], "uint16"),
+    "val": ("sbuf", [128, 48], "float32"),
+    "win": ("sbuf", [128, DUM + 384], "float32"),
+    "tt": ("sbuf", [128, 64], "float32"),
+    "land": ("sbuf", [128, 8 * N], "bfloat16"),
+    "pf": ("sbuf", [128, 2], "float32"),
+    "ini": ("sbuf", [128, 2], "float32"),
+    "dl": ("sbuf", [128, N], "float32"),
+    "me": ("sbuf", [128, 4], "int32"),
+    "mi": ("sbuf", [128, 4], "int32"),
+    "m4": ("sbuf", [128, 4], "float32"),
+    "sc0": ("sbuf", [128, N], "float32"),
+    "sc1": ("sbuf", [128, N], "float32"),
     "in2": ("sbuf", [128, 32], "float32"),
     "t2": ("sbuf", [128, 32], "float32"),
+    "l2": ("sbuf", [128, 32], "float32"),
     "e2": ("sbuf", [128, 32], "float32"),
     "f2": ("sbuf", [128, 32], "float32"),
     "pick": ("sbuf", [128, 16], "uint16"),
 }
-SEMAPHORES = ["sx", "sb", "sw", "sw2", "gw", "sp", "mo", "gi", "gn", "v", "qx", "qb", "qw0", "qw1", "qw2", "al", "ac", "asc", "loc",
-              "ofs", "offr", "pkv", "pks", "mm0", "mm1", "mm2", "mm3", "c0", "c1", "c2", "c3", "sy"]
+SEMAPHORES = ["sx", "sb", "sw", "sw2", "gw", "sp", "gi", "gn", "v", "qx", "qb", "qw0", "qw1", "qw2", "al", "ac", "asc", "loc",
+              "ofs", "cm", "sc", "ma", "offr", "pkv", "pks", "mm0", "mm1", "mm2", "mm3", "c0", "c1", "c2", "c3", "sy"]
 
 
 def rank_program(g, core, T, topo):
@@ -64,10 +62,12 @@ def rank_program(g, core, T, topo):
     V, S, P, Y = g.vector, g.scalar, g.tensor, g.sync
     Copy = ActivationFunctionType.Copy
 
-    S.dma_start(T.own[0:96, 0:1], T.pl[:]).then_inc(s.sp, 16)
+    Y.dma_start(T.own[0:32, :], T.pl[:]).then_inc(s.sp, 16)
+    for a in (1, 2, 3):
+        S.dma_start(T.own[32 * a:32 * a + 32, :], T.pl[:]).then_inc(s.sp, 16)
     Y.dma_start(T.xt[:, 0:4 * K], T.x[:]).then_inc(s.sx, 16)
-    Y.dma_start(T.bt[:], T.b[:]).then_inc(s.sb, 16)
-    S.dma_start(T.wt[:, 0:512], T.w[:, 0:512]).then_inc(s.sw, 16)
+    S.dma_start(T.bt[:], T.b[:]).then_inc(s.sb, 16)
+    Y.dma_start(T.wt[:, 0:512], T.w[:, 0:512]).then_inc(s.sw, 16)
     Y.wait_ge(s.gw, 1)
     Y.dma_start(T.wt[:, 512:1536], T.w[:, 512:1536]).then_inc(s.sw2, 16)
 
@@ -80,9 +80,11 @@ def rank_program(g, core, T, topo):
     def vw():
         V.wait_ge(s.v, n[0])
 
-    g.iota(T.pi[:], [[0, 1]], 0, 1).then_inc(s.gi, 1)
-    g.iota(T.qf[:], [[1, 16]], 0, 1, allow_small_or_imprecise_dtypes=True).then_inc(s.gn, 1)
-    g.iota(T.win[:], [[1, B + DUM]], 0, 0, allow_small_or_imprecise_dtypes=True).then_inc(s.gn, 1)
+    imprecise = {"allow_small_or_imprecise_dtypes": True}
+    g.iota(T.nd[:], [[-128, 3]], -DUM, -1).then_inc(s.gi, 1)
+    g.iota(T.val[:], [[16, 3], [1, 8], [48, 2]], -15, 1, **imprecise).then_inc(s.gi, 1)
+    g.iota(T.me[:], [[-16, 4]], 64, 1).then_inc(s.gn, 1)
+    g.iota(T.pf[:], [[128, 2]], -160, 1, **imprecise).then_inc(s.gn, 1)
 
     others = [(r + 1 + i) % N for i in range(N - 1)]
     ids, mask = [], None
@@ -98,88 +100,85 @@ def rank_program(g, core, T, topo):
                            local_sem=s.loc)
 
     ds = [(o - r) % N for o in others]
+    me = 8 * (N - 1)
     g.wait_ge(s.ofs, 1)
-    send(T.offo[:, 0:1], [T.land[:, 2 * (N - 1 - d):2 * (N - 1 - d) + 1] for d in ds], s.al)
+    send(T.land[:, me:me + 2], [T.land[:, 8 * (N - 1 - d):8 * (N - 1 - d) + 2] for d in ds], s.al)
     g.wait_ge(s.qx, 1)
     send(T.q[:, OWN:WIDE].bitcast(dt.uint8), [T.q[:, slot(d):slot(d) + K].bitcast(dt.uint8) for d in ds], s.ac)
     send(T.sq[:, OWN:WIDE], [T.sq[:, slot(d):slot(d) + K] for d in ds], s.asc)
     g.sem_inc(s.gw, 1)
 
-    V.memset(T.own[96:128, 0:1], -1).then_inc(s.mo, 1)
+    for a in range(4):
+        v(V.memset(T.sh[32 * a:32 * a + 32, :], 96.0 - 32 * a))
+    v(V.memset(T.win[:, 96:256], NONE))
     v(V.memset(T.xt[:, 4 * K:512], 0.0))
-    v(V.memset(T.in2[:], 0.0))
-    V.wait_ge(s.gi, 1)
-    v(V.tensor_scalar(T.lo[:], T.pi[:], 15, None, A.bitwise_and))
-    v(V.tensor_scalar(T.m0[:], T.pi[:], 16, None, A.is_lt))
-    v(V.tensor_scalar(T.m1[:], T.pi[:], 16, None, A.is_ge))
+    v(V.memset(T.in2[0:64, :], 0.0))
     vw()
-    v(V.tensor_scalar(T.dcol[:], T.lo[:], B + 1.0, None, A.add))
-    v(V.tensor_copy(T.lof[:], T.lo[:]))
+    V.wait_ge(s.gi, 2)
+    V.wait_ge(s.sp, 64)
+    v(V.tensor_scalar(T.u[:], T.own[:], T.sh[:], None, A.add))
+    v(V.tensor_tensor(T.vd[:], T.own[:], T.nd[:], A.mult))
     vw()
-    V.wait_ge(s.mo, 1)
-    V.wait_ge(s.sp, 16)
-    v(V.tensor_scalar(T.nego[:, 0:1], T.own[:, 0:1], 0.0, T.dcol[:], A.is_lt, A.mult))
+    v(V.tensor_tensor(T.off[:, 0:3], T.u[:], T.vd[:], A.max))
     vw()
-    V.tensor_scalar(T.offo[:, 0:1], T.own[:, 0:1], T.nego[:, 0:1], None, A.add).then_inc(s.ofs, 1)
+    v(V.tensor_copy(T.win[:].indirect(T.off[:, 0:3]), T.val[:]))
+    scat = n[0]
     V.wait_ge(s.sx, 16)
     V.quantize_mx(T.q[:, OWN:ALL], T.sq[:, OWN:ALL], T.xt[:]).then_inc(s.qx, 1)
+    V.wait_ge(s.v, scat)
+    v(V.transpose(T.tt[:, 0:32], T.win[:, 96:128]))
+    v(V.transpose(T.tt[:, 32:64], T.win[:, 224:256]))
+    vw()
+    V.tensor_tensor(T.land[:, me:me + 2], T.tt[:, 15:64:32], T.tt[:, 23:64:32], A.max).then_inc(s.ofs, 1)
 
     V.wait_ge(s.gn, 2)
-    v(V.tensor_scalar(T.qn[:], T.qf[:], T.lof[:], None, A.subtract))
+    v(V.tensor_scalar(T.mi[:], T.me[:], 48, None, A.bitwise_and))
+    v(V.memset(T.dl[:, 0:N - 1], float(-K)))
+    v(V.tensor_scalar(T.dl[:, N - 1:N], T.sh[:], 640.0, None, A.add))
+    v(V.tensor_scalar(T.ini[:], T.pf[:], T.sh[:], None, A.subtract))
     vw()
-    v(V.tensor_scalar(T.nf[:], T.qn[:], 1.0 / 6, -5.0 / 12, A.mult, A.add))
-    v(V.tensor_scalar(T.kq[:], T.qn[:], 16.0, None, A.mult))
-    vw()
-    v(V.tensor_copy(T.ni[:], T.nf[:]))
-    vw()
-    v(V.tensor_scalar(T.qf[:], T.ni[:], 95.0, None, A.mult))
-    vw()
-    v(V.tensor_tensor(T.kv[:], T.kq[:], T.qf[:], A.subtract))
-    vw()
-    for j in range(N):
-        v(V.tensor_scalar(T.val[:, 16 * j:16 * j + 16], T.kv[:], float(slot(N - 1 - j)), None, A.add))
+    V.tensor_scalar(T.m4[:], T.mi[:], 0.0, None, A.is_equal).then_inc(s.cm, 1)
     V.wait_ge(s.sb, 16)
     V.quantize_mx(T.q[:, 0:B], T.sq[:, 0:B], T.bt[:]).then_inc(s.qb, 1)
     V.wait_ge(s.sw, 16)
     V.quantize_mx(T.wq[:, 0:128], T.wsq[:, 0:128], T.wt[:, 0:512]).then_inc(s.qw0, 1)
 
-    vw()
+    V.wait_ge(s.cm, 1)
     V.wait_ge(s.ofs, 1)
     V.wait_ge(s.al, eng * (N - 1))
-    for j in range(N):
-        o = T.land[:, 2 * j:2 * j + 1] if j < N - 1 else T.offo[:, 0:1]
-        v(V.tensor_copy(T.win[:].indirect(o), T.val[:, 16 * j:16 * j + 16]))
-        vw()
-    v(V.transpose(T.tt[:], T.win[:, 0:B]))
+    V.tensor_tensor_scan(T.sc1[:], T.land[:, 1:8 * N:8], T.dl[:], T.ini[:, 1:2], A.max, A.add).then_inc(s.sc, 1)
+    v(V.tensor_tensor_scan(T.sc0[:], T.land[:, 0:8 * N:8], T.dl[:], T.ini[:, 0:1], A.max, A.add))
+    S.wait_ge(s.cm, 1)
+    S.wait_ge(s.sc, 1)
     vw()
-    v(V.tensor_tensor(T.l1[0:64, :], T.tt[0:64, 0:B:16], T.tt[64:128, 0:B:16], A.max))
+    for h in (0, 1):
+        half = slice(64 * h, 64 * h + 64)
+        S.activation(T.in2[0:64, 8 + 4 * h:12 + 4 * h], T.m4[half, :], Copy, scale=T.sc1[half, N - 1:N]).then_inc(s.ma, 1)
+        v(V.tensor_scalar(T.in2[0:64, 4 * h:4 * h + 4], T.m4[half, :], T.sc0[half, N - 1:N], None, A.mult))
     vw()
-    v(V.tensor_tensor(T.l2[0:32, :], T.l1[0:32, :], T.l1[32:64, :], A.max))
+    V.wait_ge(s.ma, 2)
+    v(V.transpose(T.t2[0:64, :], T.in2[0:64, :]))
     vw()
-    v(V.tensor_tensor(T.l3[0:32, :], T.l2[0:32, 0:16:2], T.l2[0:32, 1:16:2], A.max))
+    for a in (0, 32):
+        v(V.tensor_tensor(T.l2[a:a + 32, :], T.t2[0:32, :], T.t2[32:64, :], A.max))
     vw()
-    v(V.tensor_scalar(T.in2[0:32, 0:16:2], T.l3[0:32, :], T.m0[0:32, :], None, A.mult))
-    v(V.tensor_scalar(T.in2[0:32, 1:16:2], T.l3[0:32, :], T.m1[0:32, :], None, A.mult))
+    for a in (0, 16):
+        v(V.tensor_tensor(T.e2[0:64, a:a + 16], T.l2[0:64, 0:16], T.l2[0:64, 16:32], A.max))
     vw()
-    v(V.transpose(T.t2[0:32, :], T.in2[0:32, :]))
+    v(V.transpose(T.f2[0:64, :], T.e2[0:64, :]))
     vw()
-    v(V.tensor_tensor(T.e2[0:32, 0:16], T.t2[0:32, 0:16], T.t2[0:32, 16:32], A.max))
-    v(V.tensor_tensor(T.e2[0:32, 16:32], T.t2[0:32, 0:16], T.t2[0:32, 16:32], A.max))
-    vw()
-    v(V.transpose(T.f2[0:32, :], T.e2[0:32, :]))
-    vw()
-    for a in range(4):
-        V.tensor_copy(T.pick[32 * a:32 * a + 32, :], T.f2[0:32, 0:16]).then_inc(s.offr, 1)
+    for a in (0, 64):
+        V.tensor_copy(T.pick[a:a + 64, :], T.f2[0:64, 0:16]).then_inc(s.offr, 1)
 
     V.wait_ge(s.qx, 1)
     V.wait_ge(s.qb, 1)
     V.wait_ge(s.ac, eng * (N - 1))
-    V.wait_ge(s.offr, 4)
+    V.wait_ge(s.offr, 2)
     V.tensor_copy(T.m[:].bitcast(dt.uint32), T.q[:, 0:WIDE].bitcast(dt.uint32).indirect(T.pick[:])).then_inc(s.pkv, 1)
     S.wait_ge(s.qx, 1)
     S.wait_ge(s.qb, 1)
     S.wait_ge(s.asc, eng * (N - 1))
-    S.wait_ge(s.offr, 4)
+    S.wait_ge(s.offr, 2)
     S.activation(T.ms[:], T.sq[:, 0:WIDE].indirect(T.pick[:]), Copy).then_inc(s.pks, 1)
     V.wait_ge(s.sw2, 16)
     for o in (1, 2):

@@ -5,7 +5,7 @@ N, B, K, O = 6, 256, 96, 3
 OWN = B + K * (N - 1)
 WIDE = OWN + K
 ALL = OWN + 128
-DUM = B + 96
+DUM = B + 192
 NONE = -1024.0
 
 
@@ -24,7 +24,7 @@ SCRATCH = {
     "m": ("sbuf", [128, B], "float8_e4m3fn_x4"),
     "ms": ("sbuf", [128, B], "uint8"),
     "ys": ("sbuf", [128, O * B], "float32"),
-    "ps": ("psum", [128, 2048], "float32"),
+    "ps": ("psum", [128, 3072], "float32"),
     "own": ("sbuf", [128, 3], "int32"),
     "nd": ("sbuf", [128, 3], "int32"),
     "sh": ("sbuf", [128, 1], "float32"),
@@ -38,20 +38,16 @@ SCRATCH = {
     "pf": ("sbuf", [128, 2], "float32"),
     "ini": ("sbuf", [128, 2], "float32"),
     "dl": ("sbuf", [128, N], "float32"),
-    "me": ("sbuf", [128, 4], "int32"),
-    "mi": ("sbuf", [128, 4], "int32"),
-    "m4": ("sbuf", [128, 4], "float32"),
-    "sc0": ("sbuf", [128, N], "float32"),
-    "sc1": ("sbuf", [128, N], "float32"),
+    "sc": ("sbuf", [128, 2 * N], "float32"),
     "in2": ("sbuf", [128, 32], "float32"),
     "t2": ("sbuf", [128, 32], "float32"),
-    "l2": ("sbuf", [128, 32], "float32"),
-    "e2": ("sbuf", [128, 32], "float32"),
-    "f2": ("sbuf", [128, 32], "float32"),
+    "e2": ("sbuf", [128, 64], "float32"),
+    "f2": ("sbuf", [128, 64], "float32"),
     "pick": ("sbuf", [128, 16], "uint16"),
 }
-SEMAPHORES = ["sx", "sb", "sw", "sw2", "gw", "sp", "gi", "gn", "v", "qx", "qb", "qw0", "qw1", "qw2", "al", "ac", "asc", "loc",
-              "ofs", "cm", "sc", "ma", "offr", "pkv", "pks", "mm0", "mm1", "mm2", "mm3", "c0", "c1", "c2", "c3", "sy"]
+SEMAPHORES = ["sx", "sb", "sw", "sw2", "gl", "gw", "sp", "gi", "gn", "v", "qx", "qb", "qw0", "qw1", "qw2", "al", "ac", "asc", "loc",
+              "ofs", "shs", "cs", "ms0", "scn", "ga", "t1", "ea", "offr", "pkv0", "pkv1", "pks0", "pks1", "sy"]
+SEMAPHORES += ["mm%d" % i for i in range(6)] + ["c%d" % i for i in range(6)]
 
 
 def rank_program(g, core, T, topo):
@@ -60,13 +56,13 @@ def rank_program(g, core, T, topo):
         return
     A, s = AluOpType, T.sem
     V, S, P, Y = g.vector, g.scalar, g.tensor, g.sync
-    Copy = ActivationFunctionType.Copy
+    Copy, Identity = ActivationFunctionType.Copy, ActivationFunctionType.Identity
 
-    Y.dma_start(T.own[0:32, :], T.pl[:]).then_inc(s.sp, 16)
-    for a in (1, 2, 3):
-        S.dma_start(T.own[32 * a:32 * a + 32, :], T.pl[:]).then_inc(s.sp, 16)
+    for a, e in ((0, Y), (1, Y), (2, S), (3, S)):
+        e.dma_start(T.own[32 * a:32 * a + 32, :], T.pl[:]).then_inc(s.sp, 16)
     Y.dma_start(T.xt[:, 0:4 * K], T.x[:]).then_inc(s.sx, 16)
     S.dma_start(T.bt[:], T.b[:]).then_inc(s.sb, 16)
+    Y.wait_ge(s.gl, 1)
     Y.dma_start(T.wt[:, 0:512], T.w[:, 0:512]).then_inc(s.sw, 16)
     Y.wait_ge(s.gw, 1)
     Y.dma_start(T.wt[:, 512:1536], T.w[:, 512:1536]).then_inc(s.sw2, 16)
@@ -83,8 +79,7 @@ def rank_program(g, core, T, topo):
     imprecise = {"allow_small_or_imprecise_dtypes": True}
     g.iota(T.nd[:], [[-128, 3]], -DUM, -1).then_inc(s.gi, 1)
     g.iota(T.val[:], [[16, 3], [1, 8], [48, 2]], -15, 1, **imprecise).then_inc(s.gi, 1)
-    g.iota(T.me[:], [[-16, 4]], 64, 1).then_inc(s.gn, 1)
-    g.iota(T.pf[:], [[128, 2]], -160, 1, **imprecise).then_inc(s.gn, 1)
+    g.iota(T.pf[:], [[32, 2]], -64, 1, **imprecise).then_inc(s.gn, 1)
 
     others = [(r + 1 + i) % N for i in range(N - 1)]
     ids, mask = [], None
@@ -103,17 +98,20 @@ def rank_program(g, core, T, topo):
     me = 8 * (N - 1)
     g.wait_ge(s.ofs, 1)
     send(T.land[:, me:me + 2], [T.land[:, 8 * (N - 1 - d):8 * (N - 1 - d) + 2] for d in ds], s.al)
+    g.sem_inc(s.gl, 1)
     g.wait_ge(s.qx, 1)
     send(T.q[:, OWN:WIDE].bitcast(dt.uint8), [T.q[:, slot(d):slot(d) + K].bitcast(dt.uint8) for d in ds], s.ac)
     send(T.sq[:, OWN:WIDE], [T.sq[:, slot(d):slot(d) + K] for d in ds], s.asc)
     g.sem_inc(s.gw, 1)
 
     for a in range(4):
-        v(V.memset(T.sh[32 * a:32 * a + 32, :], 96.0 - 32 * a))
-    v(V.memset(T.win[:, 96:256], NONE))
+        V.memset(T.sh[32 * a:32 * a + 32, :], 192.0 - 64 * a).then_inc(s.shs, 1)
+    v(V.memset(T.win[:, 192:256], NONE))
     v(V.memset(T.xt[:, 4 * K:512], 0.0))
-    v(V.memset(T.in2[0:64, :], 0.0))
+    V.memset(T.in2[0:32, :], 0.0).then_inc(s.ms0, 1)
+    V.memset(T.dl[:, 0:N - 1], float(-K)).then_inc(s.cs, 1)
     vw()
+    V.wait_ge(s.shs, 4)
     V.wait_ge(s.gi, 2)
     V.wait_ge(s.sp, 64)
     v(V.tensor_scalar(T.u[:], T.own[:], T.sh[:], None, A.add))
@@ -122,89 +120,89 @@ def rank_program(g, core, T, topo):
     v(V.tensor_tensor(T.off[:, 0:3], T.u[:], T.vd[:], A.max))
     vw()
     v(V.tensor_copy(T.win[:].indirect(T.off[:, 0:3]), T.val[:]))
-    scat = n[0]
-    V.wait_ge(s.sx, 16)
-    V.quantize_mx(T.q[:, OWN:ALL], T.sq[:, OWN:ALL], T.xt[:]).then_inc(s.qx, 1)
-    V.wait_ge(s.v, scat)
-    v(V.transpose(T.tt[:, 0:32], T.win[:, 96:128]))
-    v(V.transpose(T.tt[:, 32:64], T.win[:, 224:256]))
+    vw()
+    v(V.transpose(T.tt[:], T.win[:, 192:256]))
     vw()
     V.tensor_tensor(T.land[:, me:me + 2], T.tt[:, 15:64:32], T.tt[:, 23:64:32], A.max).then_inc(s.ofs, 1)
-
-    V.wait_ge(s.gn, 2)
-    v(V.tensor_scalar(T.mi[:], T.me[:], 48, None, A.bitwise_and))
-    v(V.memset(T.dl[:, 0:N - 1], float(-K)))
-    v(V.tensor_scalar(T.dl[:, N - 1:N], T.sh[:], 640.0, None, A.add))
-    v(V.tensor_scalar(T.ini[:], T.pf[:], T.sh[:], None, A.subtract))
-    vw()
-    V.tensor_scalar(T.m4[:], T.mi[:], 0.0, None, A.is_equal).then_inc(s.cm, 1)
+    V.wait_ge(s.sx, 16)
+    V.quantize_mx(T.q[:, OWN:ALL], T.sq[:, OWN:ALL], T.xt[:]).then_inc(s.qx, 1)
     V.wait_ge(s.sb, 16)
     V.quantize_mx(T.q[:, 0:B], T.sq[:, 0:B], T.bt[:]).then_inc(s.qb, 1)
-    V.wait_ge(s.sw, 16)
-    V.quantize_mx(T.wq[:, 0:128], T.wsq[:, 0:128], T.wt[:, 0:512]).then_inc(s.qw0, 1)
 
-    V.wait_ge(s.cm, 1)
+    S.wait_ge(s.shs, 4)
+    S.wait_ge(s.gn, 1)
+    S.activation(T.dl[:, N - 1:N], T.sh[:], Copy, bias=640.0, scale=0.5).then_inc(s.cs, 1)
+    for t in (0, 1):
+        S.activation(T.ini[:, t:t + 1], T.sh[:], Identity, bias=T.pf[:, t:t + 1], scale=-1.0).then_inc(s.cs, 1)
+
+    V.wait_ge(s.cs, 4)
+    V.wait_ge(s.ms0, 1)
+    S.wait_ge(s.ms0, 1)
     V.wait_ge(s.ofs, 1)
     V.wait_ge(s.al, eng * (N - 1))
-    V.tensor_tensor_scan(T.sc1[:], T.land[:, 1:8 * N:8], T.dl[:], T.ini[:, 1:2], A.max, A.add).then_inc(s.sc, 1)
-    v(V.tensor_tensor_scan(T.sc0[:], T.land[:, 0:8 * N:8], T.dl[:], T.ini[:, 0:1], A.max, A.add))
-    S.wait_ge(s.cm, 1)
-    S.wait_ge(s.sc, 1)
+    for t in (0, 1):
+        V.tensor_tensor_scan(T.sc[:, N * t:N * t + N], T.land[:, t:8 * N:8], T.dl[:], T.ini[:, t:t + 1], A.max, A.add).then_inc(s.scn, 1)
+    V.wait_ge(s.scn, 2)
+    S.wait_ge(s.scn, 2)
+    for a in range(4):
+        out, src = T.in2[0:32, 2 * a:2 * a + 2], T.sc[32 * a:32 * a + 32, N - 1:2 * N:N]
+        if a < 2:
+            v(V.tensor_copy(out, src))
+        else:
+            S.activation(out, src, Copy).then_inc(s.ga, 1)
     vw()
-    for h in (0, 1):
-        half = slice(64 * h, 64 * h + 64)
-        S.activation(T.in2[0:64, 8 + 4 * h:12 + 4 * h], T.m4[half, :], Copy, scale=T.sc1[half, N - 1:N]).then_inc(s.ma, 1)
-        v(V.tensor_scalar(T.in2[0:64, 4 * h:4 * h + 4], T.m4[half, :], T.sc0[half, N - 1:N], None, A.mult))
-    vw()
-    V.wait_ge(s.ma, 2)
-    v(V.transpose(T.t2[0:64, :], T.in2[0:64, :]))
-    vw()
-    for a in (0, 32):
-        v(V.tensor_tensor(T.l2[a:a + 32, :], T.t2[0:32, :], T.t2[32:64, :], A.max))
-    vw()
+    V.wait_ge(s.ga, 2)
+    V.transpose(T.t2[0:32, :], T.in2[0:32, :]).then_inc(s.t1, 1)
+    V.wait_ge(s.t1, 1)
+    S.wait_ge(s.t1, 1)
     for a in (0, 16):
-        v(V.tensor_tensor(T.e2[0:64, a:a + 16], T.l2[0:64, 0:16], T.l2[0:64, 16:32], A.max))
+        v(V.tensor_copy(T.e2[0:32, a:a + 16], T.t2[0:32, 0:16]))
+        S.activation(T.e2[0:32, 32 + a:48 + a], T.t2[0:32, 16:32], Copy).then_inc(s.ea, 1)
     vw()
-    v(V.transpose(T.f2[0:64, :], T.e2[0:64, :]))
+    v(V.transpose(T.f2[0:32, 0:64:2], T.e2[0:32, 0:32]))
+    V.wait_ge(s.ea, 2)
+    v(V.transpose(T.f2[0:32, 1:64:2], T.e2[0:32, 32:64]))
     vw()
-    for a in (0, 64):
-        V.tensor_copy(T.pick[a:a + 64, :], T.f2[0:64, 0:16]).then_inc(s.offr, 1)
+    for a in range(4):
+        V.tensor_copy(T.pick[32 * a:32 * a + 32, :], T.f2[0:32, 0:16]).then_inc(s.offr, 1)
+    V.wait_ge(s.sw, 16)
+    V.quantize_mx(T.wq[:, 0:128], T.wsq[:, 0:128], T.wt[:, 0:512]).then_inc(s.qw0, 1)
 
     V.wait_ge(s.qx, 1)
     V.wait_ge(s.qb, 1)
     V.wait_ge(s.ac, eng * (N - 1))
-    V.wait_ge(s.offr, 2)
-    V.tensor_copy(T.m[:].bitcast(dt.uint32), T.q[:, 0:WIDE].bitcast(dt.uint32).indirect(T.pick[:])).then_inc(s.pkv, 1)
+    V.wait_ge(s.offr, 4)
     S.wait_ge(s.qx, 1)
     S.wait_ge(s.qb, 1)
     S.wait_ge(s.asc, eng * (N - 1))
-    S.wait_ge(s.offr, 2)
-    S.activation(T.ms[:], T.sq[:, 0:WIDE].indirect(T.pick[:]), Copy).then_inc(s.pks, 1)
+    S.wait_ge(s.offr, 4)
+    for h in (0, 1):
+        o = T.pick[:, 8 * h:8 * h + 8]
+        V.tensor_copy(T.m[:, 128 * h:128 * h + 128].bitcast(dt.uint32), T.q[:, 0:WIDE].bitcast(dt.uint32).indirect(o)).then_inc(s["pkv%d" % h], 1)
+        S.activation(T.ms[:, 128 * h:128 * h + 128], T.sq[:, 0:WIDE].indirect(o), Copy).then_inc(s["pks%d" % h], 1)
     V.wait_ge(s.sw2, 16)
     for o in (1, 2):
         V.quantize_mx(T.wq[:, 128 * o:128 * o + 128], T.wsq[:, 128 * o:128 * o + 128],
                       T.wt[:, 512 * o:512 * o + 512]).then_inc(s["qw%d" % o], 1)
 
-    P.wait_ge(s.pkv, 1)
-    P.wait_ge(s.pks, 1)
-    parts = [(0, 0, 256, S), (1, 0, 256, V), (2, 0, 128, S), (2, 128, 128, V)]
-    for i in range(4):
-        o, a, w, _ = parts[i]
+    for o in range(O):
         P.wait_ge(s["qw%d" % o], 1)
-        P.matmul_mx(T.ps[:, 512 * i:512 * i + w], T.wq[:, 128 * o:128 * o + 128], T.wsq[:, 128 * o:128 * o + 128],
-                    T.m[:, a:a + w], T.ms[:, a:a + w], True, True).then_inc(s["mm%d" % i], 1)
-    for i in range(4):
-        o, a, w, e = parts[i]
+        for h in (0, 1):
+            i = 2 * o + h
+            if o == 0:
+                P.wait_ge(s["pkv%d" % h], 1)
+                P.wait_ge(s["pks%d" % h], 1)
+            P.matmul_mx(T.ps[:, 512 * i:512 * i + 128], T.wq[:, 128 * o:128 * o + 128], T.wsq[:, 128 * o:128 * o + 128],
+                        T.m[:, 128 * h:128 * h + 128], T.ms[:, 128 * h:128 * h + 128], True, True).then_inc(s["mm%d" % i], 1)
+    for i in range(6):
+        e = V if i in (2, 4) else S
         e.wait_ge(s["mm%d" % i], 1)
-        out, src = T.ys[:, 256 * o + a:256 * o + a + w], T.ps[:, 512 * i:512 * i + w]
+        out, src = T.ys[:, 128 * i:128 * i + 128], T.ps[:, 512 * i:512 * i + 128]
         (V.tensor_copy(out, src) if e is V else S.activation(out, src, Copy)).then_inc(s["c%d" % i], 1)
-    Y.wait_ge(s.c0, 1)
-    Y.dma_start(T.y[:, 0:256], T.ys[:, 0:256]).then_inc(s.sy, 16)
-    Y.wait_ge(s.c1, 1)
-    Y.dma_start(T.y[:, 256:512], T.ys[:, 256:512]).then_inc(s.sy, 16)
-    Y.wait_ge(s.c2, 1)
-    Y.wait_ge(s.c3, 1)
-    Y.dma_start(T.y[:, 512:768], T.ys[:, 512:768]).then_inc(s.sy, 16)
+    for o in range(O):
+        Y.wait_ge(s["c%d" % (2 * o)], 1)
+        Y.wait_ge(s["c%d" % (2 * o + 1)], 1)
+        Y.dma_start(T.y[:, 256 * o:256 * o + 256], T.ys[:, 256 * o:256 * o + 256]).then_inc(s.sy, 16)
     Y.wait_ge(s.sy, 48)
     V.wait_ge(s.v, n[0])
     g.wait_ge(s.loc, 3 * eng)

@@ -38,15 +38,16 @@ SCRATCH = {
     "pf": ("sbuf", [128, 2], "float32"),
     "ini": ("sbuf", [128, 2], "float32"),
     "dl": ("sbuf", [128, N], "float32"),
+    "hm": ("sbuf", [128, 2], "float32"),
     "sc": ("sbuf", [128, 2 * N], "float32"),
     "in2": ("sbuf", [128, 32], "float32"),
-    "t2": ("sbuf", [128, 32], "float32"),
-    "e2": ("sbuf", [128, 64], "float32"),
+    "t2": ("sbuf", [128, 64], "float32"),
+    "mk": ("sbuf", [128, 16], "float32"),
     "f2": ("sbuf", [128, 64], "float32"),
     "pick": ("sbuf", [128, 16], "uint16"),
 }
-SEMAPHORES = ["sx", "sb", "sw", "sw2", "gl", "gw", "sp", "gi", "gn", "v", "qx", "qb", "qw0", "qw1", "qw2", "al", "ac", "asc", "loc",
-              "ofs", "shs", "cs", "ms0", "scn", "ga", "t1", "ea", "offr", "pkv0", "pkv1", "pks0", "pks1", "sy"]
+SEMAPHORES = ["sx", "sb", "sw", "sw2", "gw", "sp", "gi", "gn", "v", "qx", "qb", "qw0", "qw1", "qw2", "al", "ac", "asc", "loc",
+              "ofs", "shs", "cs", "ms0", "scn", "cp", "hms", "mks", "offr", "pkv0", "pkv1", "pks0", "pks1", "sy"]
 SEMAPHORES += ["mm%d" % i for i in range(6)] + ["c%d" % i for i in range(6)]
 
 
@@ -61,8 +62,7 @@ def rank_program(g, core, T, topo):
     for a, e in ((0, Y), (1, Y), (2, S), (3, S)):
         e.dma_start(T.own[32 * a:32 * a + 32, :], T.pl[:]).then_inc(s.sp, 16)
     Y.dma_start(T.xt[:, 0:4 * K], T.x[:]).then_inc(s.sx, 16)
-    S.dma_start(T.bt[:], T.b[:]).then_inc(s.sb, 16)
-    Y.wait_ge(s.gl, 1)
+    Y.dma_start(T.bt[:], T.b[:]).then_inc(s.sb, 16)
     Y.dma_start(T.wt[:, 0:512], T.w[:, 0:512]).then_inc(s.sw, 16)
     Y.wait_ge(s.gw, 1)
     Y.dma_start(T.wt[:, 512:1536], T.w[:, 512:1536]).then_inc(s.sw2, 16)
@@ -89,27 +89,28 @@ def rank_program(g, core, T, topo):
         k = topo.mask(core, T.cores[o])
         mask = k if mask is None else mask & k
     eng = len([e for e in topo.engines(core, T.cores[others[0]])])
-
-    def send(src, dsts, sem):
-        g.remote_dma_fused([RemoteDMATransfer(dst_ids=ids, dma_engine_mask=mask, remote_sem=sem, srcs=[src], dsts=dsts)],
-                           local_sem=s.loc)
-
     ds = [(o - r) % N for o in others]
+
+    def send(src, dst, sem, a=0, b=N - 1):
+        g.remote_dma_fused([RemoteDMATransfer(dst_ids=ids[a:b], dma_engine_mask=mask, remote_sem=sem, srcs=[src],
+                                              dsts=[dst(d) for d in ds[a:b]])], local_sem=s.loc)
+
+    def scales(d):
+        return T.sq[:, slot(d):slot(d) + K]
+
     me = 8 * (N - 1)
-    g.wait_ge(s.ofs, 1)
-    send(T.land[:, me:me + 2], [T.land[:, 8 * (N - 1 - d):8 * (N - 1 - d) + 2] for d in ds], s.al)
-    g.sem_inc(s.gl, 1)
     g.wait_ge(s.qx, 1)
-    send(T.q[:, OWN:WIDE].bitcast(dt.uint8), [T.q[:, slot(d):slot(d) + K].bitcast(dt.uint8) for d in ds], s.ac)
-    send(T.sq[:, OWN:WIDE], [T.sq[:, slot(d):slot(d) + K] for d in ds], s.asc)
+    send(T.sq[:, OWN:WIDE], scales, s.asc, 0, 1)
+    g.wait_ge(s.ofs, 1)
+    send(T.land[:, me:me + 2], lambda d: T.land[:, 8 * (N - 1 - d):8 * (N - 1 - d) + 2], s.al)
+    send(T.q[:, OWN:WIDE].bitcast(dt.uint8), lambda d: T.q[:, slot(d):slot(d) + K].bitcast(dt.uint8), s.ac)
+    send(T.sq[:, OWN:WIDE], scales, s.asc, 1)
     g.sem_inc(s.gw, 1)
 
     for a in range(4):
         V.memset(T.sh[32 * a:32 * a + 32, :], 192.0 - 64 * a).then_inc(s.shs, 1)
     v(V.memset(T.win[:, 192:256], NONE))
     v(V.memset(T.xt[:, 4 * K:512], 0.0))
-    V.memset(T.in2[0:32, :], 0.0).then_inc(s.ms0, 1)
-    V.memset(T.dl[:, 0:N - 1], float(-K)).then_inc(s.cs, 1)
     vw()
     V.wait_ge(s.shs, 4)
     V.wait_ge(s.gi, 2)
@@ -120,24 +121,33 @@ def rank_program(g, core, T, topo):
     v(V.tensor_tensor(T.off[:, 0:3], T.u[:], T.vd[:], A.max))
     vw()
     v(V.tensor_copy(T.win[:].indirect(T.off[:, 0:3]), T.val[:]))
+    V.wait_ge(s.sx, 16)
+    V.quantize_mx(T.q[:, OWN:ALL], T.sq[:, OWN:ALL], T.xt[:]).then_inc(s.qx, 1)
     vw()
     v(V.transpose(T.tt[:], T.win[:, 192:256]))
     vw()
     V.tensor_tensor(T.land[:, me:me + 2], T.tt[:, 15:64:32], T.tt[:, 23:64:32], A.max).then_inc(s.ofs, 1)
-    V.wait_ge(s.sx, 16)
-    V.quantize_mx(T.q[:, OWN:ALL], T.sq[:, OWN:ALL], T.xt[:]).then_inc(s.qx, 1)
+    V.memset(T.in2[0:32, :], 0.0).then_inc(s.ms0, 1)
+    V.memset(T.t2[0:32, :], 0.0).then_inc(s.ms0, 1)
+    V.memset(T.dl[:, 0:N - 1], float(-K)).then_inc(s.cs, 1)
+    V.wait_ge(s.gn, 1)
+    V.tensor_scalar(T.hm[0:32, 0:1], T.pf[0:32, 0:1], -48.0, None, A.is_lt).then_inc(s.hms, 1)
+    V.tensor_scalar(T.hm[0:32, 1:2], T.pf[0:32, 0:1], -48.0, None, A.is_ge).then_inc(s.hms, 1)
     V.wait_ge(s.sb, 16)
     V.quantize_mx(T.q[:, 0:B], T.sq[:, 0:B], T.bt[:]).then_inc(s.qb, 1)
+    V.wait_ge(s.sw, 16)
+    V.quantize_mx(T.wq[:, 0:128], T.wsq[:, 0:128], T.wt[:, 0:512]).then_inc(s.qw0, 1)
 
     S.wait_ge(s.shs, 4)
     S.wait_ge(s.gn, 1)
     S.activation(T.dl[:, N - 1:N], T.sh[:], Copy, bias=640.0, scale=0.5).then_inc(s.cs, 1)
     for t in (0, 1):
         S.activation(T.ini[:, t:t + 1], T.sh[:], Identity, bias=T.pf[:, t:t + 1], scale=-1.0).then_inc(s.cs, 1)
+    S.wait_ge(s.ms0, 2)
+    S.wait_ge(s.hms, 2)
 
     V.wait_ge(s.cs, 4)
-    V.wait_ge(s.ms0, 1)
-    S.wait_ge(s.ms0, 1)
+    V.wait_ge(s.ms0, 2)
     V.wait_ge(s.ofs, 1)
     V.wait_ge(s.al, eng * (N - 1))
     for t in (0, 1):
@@ -146,27 +156,19 @@ def rank_program(g, core, T, topo):
     S.wait_ge(s.scn, 2)
     for a in range(4):
         out, src = T.in2[0:32, 2 * a:2 * a + 2], T.sc[32 * a:32 * a + 32, N - 1:2 * N:N]
-        if a < 2:
-            v(V.tensor_copy(out, src))
-        else:
-            S.activation(out, src, Copy).then_inc(s.ga, 1)
+        (V.tensor_copy(out, src) if a < 2 else S.activation(out, src, Copy)).then_inc(s.cp, 1)
+    V.wait_ge(s.cp, 4)
+    S.wait_ge(s.cp, 4)
+    v(V.transpose(T.t2[0:32, 16:48], T.in2[0:32, :]))
+    for h in (0, 1):
+        S.activation(T.mk[0:32, h:16:2], T.in2[0:32, 0:8], Identity, scale=T.hm[0:32, h:h + 1]).then_inc(s.mks, 1)
     vw()
-    V.wait_ge(s.ga, 2)
-    V.transpose(T.t2[0:32, :], T.in2[0:32, :]).then_inc(s.t1, 1)
-    V.wait_ge(s.t1, 1)
-    S.wait_ge(s.t1, 1)
-    for a in (0, 16):
-        v(V.tensor_copy(T.e2[0:32, a:a + 16], T.t2[0:32, 0:16]))
-        S.activation(T.e2[0:32, 32 + a:48 + a], T.t2[0:32, 16:32], Copy).then_inc(s.ea, 1)
+    for h in (0, 1):
+        v(V.transpose(T.f2[0:32, h:64:2], T.t2[0:32, 32 * h:32 * h + 32]))
     vw()
-    v(V.transpose(T.f2[0:32, 0:64:2], T.e2[0:32, 0:32]))
-    V.wait_ge(s.ea, 2)
-    v(V.transpose(T.f2[0:32, 1:64:2], T.e2[0:32, 32:64]))
-    vw()
+    V.wait_ge(s.mks, 2)
     for a in range(4):
-        V.tensor_copy(T.pick[32 * a:32 * a + 32, :], T.f2[0:32, 0:16]).then_inc(s.offr, 1)
-    V.wait_ge(s.sw, 16)
-    V.quantize_mx(T.wq[:, 0:128], T.wsq[:, 0:128], T.wt[:, 0:512]).then_inc(s.qw0, 1)
+        V.tensor_tensor(T.pick[32 * a:32 * a + 32, :], T.f2[0:32, 0:16], T.mk[0:32, :], A.max).then_inc(s.offr, 1)
 
     V.wait_ge(s.qx, 1)
     V.wait_ge(s.qb, 1)
@@ -199,10 +201,10 @@ def rank_program(g, core, T, topo):
         e.wait_ge(s["mm%d" % i], 1)
         out, src = T.ys[:, 128 * i:128 * i + 128], T.ps[:, 512 * i:512 * i + 128]
         (V.tensor_copy(out, src) if e is V else S.activation(out, src, Copy)).then_inc(s["c%d" % i], 1)
-    for o in range(O):
-        Y.wait_ge(s["c%d" % (2 * o)], 1)
-        Y.wait_ge(s["c%d" % (2 * o + 1)], 1)
-        Y.dma_start(T.y[:, 256 * o:256 * o + 256], T.ys[:, 256 * o:256 * o + 256]).then_inc(s.sy, 16)
-    Y.wait_ge(s.sy, 48)
+    for a, b in ((0, 1), (1, 2), (2, 4), (4, 5), (5, 6)):
+        for i in range(a, b):
+            Y.wait_ge(s["c%d" % i], 1)
+        Y.dma_start(T.y[:, 128 * a:128 * b], T.ys[:, 128 * a:128 * b]).then_inc(s.sy, 16)
+    Y.wait_ge(s.sy, 80)
     V.wait_ge(s.v, n[0])
-    g.wait_ge(s.loc, 3 * eng)
+    g.wait_ge(s.loc, 4 * eng)

@@ -46,7 +46,7 @@ SCRATCH = {
     "f2": ("sbuf", [128, 64], "float32"),
     "pick": ("sbuf", [128, 16], "uint16"),
 }
-SEMAPHORES = ["sx", "sb", "sw", "sw2", "gw", "sp", "gi", "gn", "v", "qx", "qb", "qw0", "qw1", "qw2", "al", "ac", "asc", "loc",
+SEMAPHORES = ["sx", "sb", "sw", "sw2", "sp", "gi", "gn", "v", "qx", "qb", "qw0", "qw1", "qw2", "al", "ac", "asc", "loc",
               "ofs", "shs", "cs", "ms0", "scn", "cp", "hms", "mks", "offr", "pkv0", "pkv1", "pks0", "pks1", "sy"]
 SEMAPHORES += ["mm%d" % i for i in range(6)] + ["c%d" % i for i in range(6)]
 
@@ -64,7 +64,6 @@ def rank_program(g, core, T, topo):
     Y.dma_start(T.xt[:, 0:4 * K], T.x[:]).then_inc(s.sx, 16)
     Y.dma_start(T.bt[:], T.b[:]).then_inc(s.sb, 16)
     Y.dma_start(T.wt[:, 0:512], T.w[:, 0:512]).then_inc(s.sw, 16)
-    Y.wait_ge(s.gw, 1)
     Y.dma_start(T.wt[:, 512:1536], T.w[:, 512:1536]).then_inc(s.sw2, 16)
 
     n = [0]
@@ -105,7 +104,6 @@ def rank_program(g, core, T, topo):
     send(T.land[:, me:me + 2], lambda d: T.land[:, 8 * (N - 1 - d):8 * (N - 1 - d) + 2], s.al)
     send(T.q[:, OWN:WIDE].bitcast(dt.uint8), lambda d: T.q[:, slot(d):slot(d) + K].bitcast(dt.uint8), s.ac)
     send(T.sq[:, OWN:WIDE], scales, s.asc, 1)
-    g.sem_inc(s.gw, 1)
 
     for a in range(4):
         V.memset(T.sh[32 * a:32 * a + 32, :], 192.0 - 64 * a).then_inc(s.shs, 1)
@@ -119,10 +117,10 @@ def rank_program(g, core, T, topo):
     v(V.tensor_tensor(T.vd[:], T.own[:], T.nd[:], A.mult))
     vw()
     v(V.tensor_tensor(T.off[:, 0:3], T.u[:], T.vd[:], A.max))
-    vw()
-    v(V.tensor_copy(T.win[:].indirect(T.off[:, 0:3]), T.val[:]))
     V.wait_ge(s.sx, 16)
     V.quantize_mx(T.q[:, OWN:ALL], T.sq[:, OWN:ALL], T.xt[:]).then_inc(s.qx, 1)
+    vw()
+    v(V.tensor_copy(T.win[:].indirect(T.off[:, 0:3]), T.val[:]))
     vw()
     v(V.transpose(T.tt[:], T.win[:, 192:256]))
     vw()
@@ -135,8 +133,11 @@ def rank_program(g, core, T, topo):
     V.tensor_scalar(T.hm[0:32, 1:2], T.pf[0:32, 0:1], -48.0, None, A.is_ge).then_inc(s.hms, 1)
     V.wait_ge(s.sb, 16)
     V.quantize_mx(T.q[:, 0:B], T.sq[:, 0:B], T.bt[:]).then_inc(s.qb, 1)
-    V.wait_ge(s.sw, 16)
-    V.quantize_mx(T.wq[:, 0:128], T.wsq[:, 0:128], T.wt[:, 0:512]).then_inc(s.qw0, 1)
+    for o in range(O):
+        if o < 2:
+            V.wait_ge(s.sw2 if o else s.sw, 16)
+        V.quantize_mx(T.wq[:, 128 * o:128 * o + 128], T.wsq[:, 128 * o:128 * o + 128],
+                      T.wt[:, 512 * o:512 * o + 512]).then_inc(s["qw%d" % o], 1)
 
     S.wait_ge(s.shs, 4)
     S.wait_ge(s.gn, 1)
@@ -145,10 +146,14 @@ def rank_program(g, core, T, topo):
         S.activation(T.ini[:, t:t + 1], T.sh[:], Identity, bias=T.pf[:, t:t + 1], scale=-1.0).then_inc(s.cs, 1)
     S.wait_ge(s.ms0, 2)
     S.wait_ge(s.hms, 2)
+    S.wait_ge(s.qx, 1)
+    S.wait_ge(s.qb, 1)
 
     V.wait_ge(s.cs, 4)
     V.wait_ge(s.ms0, 2)
     V.wait_ge(s.ofs, 1)
+    V.wait_ge(s.qx, 1)
+    V.wait_ge(s.qb, 1)
     V.wait_ge(s.al, eng * (N - 1))
     for t in (0, 1):
         V.tensor_tensor_scan(T.sc[:, N * t:N * t + N], T.land[:, t:8 * N:8], T.dl[:], T.ini[:, t:t + 1], A.max, A.add).then_inc(s.scn, 1)
@@ -165,46 +170,37 @@ def rank_program(g, core, T, topo):
     vw()
     for h in (0, 1):
         v(V.transpose(T.f2[0:32, h:64:2], T.t2[0:32, 32 * h:32 * h + 32]))
-    vw()
     V.wait_ge(s.mks, 2)
+    vw()
     for a in range(4):
         V.tensor_tensor(T.pick[32 * a:32 * a + 32, :], T.f2[0:32, 0:16], T.mk[0:32, :], A.max).then_inc(s.offr, 1)
 
-    V.wait_ge(s.qx, 1)
-    V.wait_ge(s.qb, 1)
     V.wait_ge(s.ac, eng * (N - 1))
     V.wait_ge(s.offr, 4)
-    S.wait_ge(s.qx, 1)
-    S.wait_ge(s.qb, 1)
     S.wait_ge(s.asc, eng * (N - 1))
     S.wait_ge(s.offr, 4)
     for h in (0, 1):
         o = T.pick[:, 8 * h:8 * h + 8]
         V.tensor_copy(T.m[:, 128 * h:128 * h + 128].bitcast(dt.uint32), T.q[:, 0:WIDE].bitcast(dt.uint32).indirect(o)).then_inc(s["pkv%d" % h], 1)
         S.activation(T.ms[:, 128 * h:128 * h + 128], T.sq[:, 0:WIDE].indirect(o), Copy).then_inc(s["pks%d" % h], 1)
-    V.wait_ge(s.sw2, 16)
-    for o in (1, 2):
-        V.quantize_mx(T.wq[:, 128 * o:128 * o + 128], T.wsq[:, 128 * o:128 * o + 128],
-                      T.wt[:, 512 * o:512 * o + 512]).then_inc(s["qw%d" % o], 1)
 
+    seq = [(h, o) for h in (0, 1) for o in range(O)]
     for o in range(O):
         P.wait_ge(s["qw%d" % o], 1)
-        for h in (0, 1):
-            i = 2 * o + h
-            if o == 0:
-                P.wait_ge(s["pkv%d" % h], 1)
-                P.wait_ge(s["pks%d" % h], 1)
-            P.matmul_mx(T.ps[:, 512 * i:512 * i + 128], T.wq[:, 128 * o:128 * o + 128], T.wsq[:, 128 * o:128 * o + 128],
-                        T.m[:, 128 * h:128 * h + 128], T.ms[:, 128 * h:128 * h + 128], True, True).then_inc(s["mm%d" % i], 1)
-    for i in range(6):
-        e = V if i in (2, 4) else S
+    for i, (h, o) in enumerate(seq):
+        if o == 0:
+            P.wait_ge(s["pkv%d" % h], 1)
+            P.wait_ge(s["pks%d" % h], 1)
+        P.matmul_mx(T.ps[:, 512 * i:512 * i + 128], T.wq[:, 128 * o:128 * o + 128], T.wsq[:, 128 * o:128 * o + 128],
+                    T.m[:, 128 * h:128 * h + 128], T.ms[:, 128 * h:128 * h + 128], True, True).then_inc(s["mm%d" % i], 1)
+    for i, (h, o) in enumerate(seq):
+        e = V if i in (0, 2, 4) else S
+        c = 256 * o + 128 * h
         e.wait_ge(s["mm%d" % i], 1)
-        out, src = T.ys[:, 128 * i:128 * i + 128], T.ps[:, 512 * i:512 * i + 128]
+        out, src = T.ys[:, c:c + 128], T.ps[:, 512 * i:512 * i + 128]
         (V.tensor_copy(out, src) if e is V else S.activation(out, src, Copy)).then_inc(s["c%d" % i], 1)
-    for a, b in ((0, 1), (1, 2), (2, 4), (4, 5), (5, 6)):
-        for i in range(a, b):
-            Y.wait_ge(s["c%d" % i], 1)
-        Y.dma_start(T.y[:, 128 * a:128 * b], T.ys[:, 128 * a:128 * b]).then_inc(s.sy, 16)
-    Y.wait_ge(s.sy, 80)
+        Y.wait_ge(s["c%d" % i], 1)
+        Y.dma_start(T.y[:, c:c + 128], T.ys[:, c:c + 128]).then_inc(s.sy, 16)
+    Y.wait_ge(s.sy, 96)
     V.wait_ge(s.v, n[0])
     g.wait_ge(s.loc, 4 * eng)

from concourse.bass import DstId, RemoteDMATransfer
from concourse.mybir import dt, AluOpType, ActivationFunctionType

N, B, K, O = 6, 256, 96, 3
OWN = B + K * (N - 1)
WIDE = OWN + K
ALL = OWN + 128
DUM = B + 192
NONE = -1024.0


def slot(d):
    return B + K * (N - 1 - d)


SCRATCH = {
    "xt": ("sbuf", [128, 512], "bfloat16"),
    "bt": ("sbuf", [128, 4 * B], "bfloat16"),
    "wt": ("sbuf", [128, 512 * O], "bfloat16"),
    "q": ("sbuf", [128, ALL], "float8_e4m3fn_x4"),
    "sq": ("sbuf", [128, ALL], "uint8"),
    "wq": ("sbuf", [128, 128 * O], "float8_e4m3fn_x4"),
    "wsq": ("sbuf", [128, 128 * O], "uint8"),
    "m": ("sbuf", [128, B], "float8_e4m3fn_x4"),
    "ms": ("sbuf", [128, B], "uint8"),
    "ys": ("sbuf", [128, O * B], "float32"),
    "ps": ("psum", [128, 3072], "float32"),
    "own": ("sbuf", [128, 3], "int32"),
    "nd": ("sbuf", [128, 3], "int32"),
    "sh": ("sbuf", [128, 1], "float32"),
    "u": ("sbuf", [128, 3], "int32"),
    "vd": ("sbuf", [128, 3], "int32"),
    "off": ("sbuf", [128, 4], "uint16"),
    "val": ("sbuf", [128, 48], "float32"),
    "win": ("sbuf", [128, DUM + 384], "float32"),
    "tt": ("sbuf", [128, 64], "float32"),
    "land": ("sbuf", [128, 8 * N], "bfloat16"),
    "pf": ("sbuf", [128, 2], "float32"),
    "ini": ("sbuf", [128, 2], "float32"),
    "dl": ("sbuf", [128, N], "float32"),
    "hm": ("sbuf", [128, 2], "float32"),
    "sc": ("sbuf", [128, 2 * N], "float32"),
    "in2": ("sbuf", [128, 32], "float32"),
    "t2": ("sbuf", [128, 64], "float32"),
    "mk": ("sbuf", [128, 16], "float32"),
    "f2": ("sbuf", [128, 64], "float32"),
    "pick": ("sbuf", [128, 16], "uint16"),
}
SEMAPHORES = ["sx", "sb", "sw", "sw2", "sp", "gi", "gn", "v", "qx", "qb", "qw0", "qw1", "qw2", "al", "ac", "asc", "loc",
              "ofs", "shs", "cs", "ms0", "scn", "cp", "hms", "mks", "offr", "pkv0", "pkv1", "pks0", "pks1", "sy"]
SEMAPHORES += ["mm%d" % i for i in range(6)] + ["c%d" % i for i in range(6)]


def rank_program(g, core, T, topo):
    r = T.rank_of(core)
    if r is None:
        return
    A, s = AluOpType, T.sem
    V, S, P, Y = g.vector, g.scalar, g.tensor, g.sync
    Copy, Identity = ActivationFunctionType.Copy, ActivationFunctionType.Identity

    for a, e in ((0, Y), (1, Y), (2, S), (3, S)):
        e.dma_start(T.own[32 * a:32 * a + 32, :], T.pl[:]).then_inc(s.sp, 16)
    Y.dma_start(T.xt[:, 0:4 * K], T.x[:]).then_inc(s.sx, 16)
    Y.dma_start(T.bt[:], T.b[:]).then_inc(s.sb, 16)
    Y.dma_start(T.wt[:, 0:512], T.w[:, 0:512]).then_inc(s.sw, 16)
    Y.dma_start(T.wt[:, 512:1536], T.w[:, 512:1536]).then_inc(s.sw2, 16)

    n = [0]

    def v(ins):
        n[0] += 1
        return ins.then_inc(s.v, 1)

    def vw():
        V.wait_ge(s.v, n[0])

    imprecise = {"allow_small_or_imprecise_dtypes": True}
    g.iota(T.nd[:], [[-128, 3]], -DUM, -1).then_inc(s.gi, 1)
    g.iota(T.val[:], [[16, 3], [1, 8], [48, 2]], -15, 1, **imprecise).then_inc(s.gi, 1)
    g.iota(T.pf[:], [[32, 2]], -64, 1, **imprecise).then_inc(s.gn, 1)

    others = [(r + 1 + i) % N for i in range(N - 1)]
    ids, mask = [], None
    for o in others:
        rid, pid, _se = topo.addr(T.cores[o])
        ids.append(DstId(rid=rid, pnc=pid))
        k = topo.mask(core, T.cores[o])
        mask = k if mask is None else mask & k
    eng = len([e for e in topo.engines(core, T.cores[others[0]])])
    ds = [(o - r) % N for o in others]

    def send(src, dst, sem, a=0, b=N - 1):
        g.remote_dma_fused([RemoteDMATransfer(dst_ids=ids[a:b], dma_engine_mask=mask, remote_sem=sem, srcs=[src],
                                              dsts=[dst(d) for d in ds[a:b]])], local_sem=s.loc)

    def scales(d):
        return T.sq[:, slot(d):slot(d) + K]

    me = 8 * (N - 1)
    g.wait_ge(s.qx, 1)
    send(T.sq[:, OWN:WIDE], scales, s.asc, 0, 1)
    g.wait_ge(s.ofs, 1)
    send(T.land[:, me:me + 2], lambda d: T.land[:, 8 * (N - 1 - d):8 * (N - 1 - d) + 2], s.al)
    send(T.q[:, OWN:WIDE].bitcast(dt.uint8), lambda d: T.q[:, slot(d):slot(d) + K].bitcast(dt.uint8), s.ac)
    send(T.sq[:, OWN:WIDE], scales, s.asc, 1)

    for a in range(4):
        V.memset(T.sh[32 * a:32 * a + 32, :], 192.0 - 64 * a).then_inc(s.shs, 1)
    v(V.memset(T.win[:, 192:256], NONE))
    v(V.memset(T.xt[:, 4 * K:512], 0.0))
    vw()
    V.wait_ge(s.shs, 4)
    V.wait_ge(s.gi, 2)
    V.wait_ge(s.sp, 64)
    v(V.tensor_scalar(T.u[:], T.own[:], T.sh[:], None, A.add))
    v(V.tensor_tensor(T.vd[:], T.own[:], T.nd[:], A.mult))
    vw()
    v(V.tensor_tensor(T.off[:, 0:3], T.u[:], T.vd[:], A.max))
    V.wait_ge(s.sx, 16)
    V.quantize_mx(T.q[:, OWN:ALL], T.sq[:, OWN:ALL], T.xt[:]).then_inc(s.qx, 1)
    vw()
    v(V.tensor_copy(T.win[:].indirect(T.off[:, 0:3]), T.val[:]))
    vw()
    v(V.transpose(T.tt[:], T.win[:, 192:256]))
    vw()
    V.tensor_tensor(T.land[:, me:me + 2], T.tt[:, 15:64:32], T.tt[:, 23:64:32], A.max).then_inc(s.ofs, 1)
    V.memset(T.in2[0:32, :], 0.0).then_inc(s.ms0, 1)
    V.memset(T.t2[0:32, :], 0.0).then_inc(s.ms0, 1)
    V.memset(T.dl[:, 0:N - 1], float(-K)).then_inc(s.cs, 1)
    V.wait_ge(s.gn, 1)
    V.tensor_scalar(T.hm[0:32, 0:1], T.pf[0:32, 0:1], -48.0, None, A.is_lt).then_inc(s.hms, 1)
    V.tensor_scalar(T.hm[0:32, 1:2], T.pf[0:32, 0:1], -48.0, None, A.is_ge).then_inc(s.hms, 1)
    V.wait_ge(s.sb, 16)
    V.quantize_mx(T.q[:, 0:B], T.sq[:, 0:B], T.bt[:]).then_inc(s.qb, 1)
    for o in range(O):
        if o < 2:
            V.wait_ge(s.sw2 if o else s.sw, 16)
        V.quantize_mx(T.wq[:, 128 * o:128 * o + 128], T.wsq[:, 128 * o:128 * o + 128],
                      T.wt[:, 512 * o:512 * o + 512]).then_inc(s["qw%d" % o], 1)

    S.wait_ge(s.shs, 4)
    S.wait_ge(s.gn, 1)
    S.activation(T.dl[:, N - 1:N], T.sh[:], Copy, bias=640.0, scale=0.5).then_inc(s.cs, 1)
    for t in (0, 1):
        S.activation(T.ini[:, t:t + 1], T.sh[:], Identity, bias=T.pf[:, t:t + 1], scale=-1.0).then_inc(s.cs, 1)
    S.wait_ge(s.ms0, 2)
    S.wait_ge(s.hms, 2)
    S.wait_ge(s.qx, 1)
    S.wait_ge(s.qb, 1)

    V.wait_ge(s.cs, 4)
    V.wait_ge(s.ms0, 2)
    V.wait_ge(s.ofs, 1)
    V.wait_ge(s.qx, 1)
    V.wait_ge(s.qb, 1)
    V.wait_ge(s.al, eng * (N - 1))
    for t in (0, 1):
        V.tensor_tensor_scan(T.sc[:, N * t:N * t + N], T.land[:, t:8 * N:8], T.dl[:], T.ini[:, t:t + 1], A.max, A.add).then_inc(s.scn, 1)
    V.wait_ge(s.scn, 2)
    S.wait_ge(s.scn, 2)
    for a in range(4):
        out, src = T.in2[0:32, 2 * a:2 * a + 2], T.sc[32 * a:32 * a + 32, N - 1:2 * N:N]
        (V.tensor_copy(out, src) if a < 2 else S.activation(out, src, Copy)).then_inc(s.cp, 1)
    V.wait_ge(s.cp, 4)
    S.wait_ge(s.cp, 4)
    v(V.transpose(T.t2[0:32, 16:48], T.in2[0:32, :]))
    for h in (0, 1):
        S.activation(T.mk[0:32, h:16:2], T.in2[0:32, 0:8], Identity, scale=T.hm[0:32, h:h + 1]).then_inc(s.mks, 1)
    vw()
    for h in (0, 1):
        v(V.transpose(T.f2[0:32, h:64:2], T.t2[0:32, 32 * h:32 * h + 32]))
    V.wait_ge(s.mks, 2)
    vw()
    for a in range(4):
        V.tensor_tensor(T.pick[32 * a:32 * a + 32, :], T.f2[0:32, 0:16], T.mk[0:32, :], A.max).then_inc(s.offr, 1)

    V.wait_ge(s.ac, eng * (N - 1))
    V.wait_ge(s.offr, 4)
    S.wait_ge(s.asc, eng * (N - 1))
    S.wait_ge(s.offr, 4)
    for h in (0, 1):
        o = T.pick[:, 8 * h:8 * h + 8]
        V.tensor_copy(T.m[:, 128 * h:128 * h + 128].bitcast(dt.uint32), T.q[:, 0:WIDE].bitcast(dt.uint32).indirect(o)).then_inc(s["pkv%d" % h], 1)
        S.activation(T.ms[:, 128 * h:128 * h + 128], T.sq[:, 0:WIDE].indirect(o), Copy).then_inc(s["pks%d" % h], 1)

    seq = [(h, o) for h in (0, 1) for o in range(O)]
    for o in range(O):
        P.wait_ge(s["qw%d" % o], 1)
    for i, (h, o) in enumerate(seq):
        if o == 0:
            P.wait_ge(s["pkv%d" % h], 1)
            P.wait_ge(s["pks%d" % h], 1)
        P.matmul_mx(T.ps[:, 512 * i:512 * i + 128], T.wq[:, 128 * o:128 * o + 128], T.wsq[:, 128 * o:128 * o + 128],
                    T.m[:, 128 * h:128 * h + 128], T.ms[:, 128 * h:128 * h + 128], True, True).then_inc(s["mm%d" % i], 1)
    for i, (h, o) in enumerate(seq):
        e = V if i in (0, 2, 4) else S
        c = 256 * o + 128 * h
        e.wait_ge(s["mm%d" % i], 1)
        out, src = T.ys[:, c:c + 128], T.ps[:, 512 * i:512 * i + 128]
        (V.tensor_copy(out, src) if e is V else S.activation(out, src, Copy)).then_inc(s["c%d" % i], 1)
        Y.wait_ge(s["c%d" % i], 1)
        Y.dma_start(T.y[:, c:c + 128], T.ys[:, c:c + 128]).then_inc(s.sy, 16)
    Y.wait_ge(s.sy, 96)
    V.wait_ge(s.v, n[0])
    g.wait_ge(s.loc, 4 * eng)
